import numpy as np
import ml_dtypes

BF16 = ml_dtypes.bfloat16


def bf(x):
    return np.asarray(x, np.float32).astype(BF16)


def f32(x):
    return np.asarray(x, np.float32)


def f64(x):
    return np.asarray(x).astype(np.float64)


def striped(idx):
    return np.tile(idx.reshape(-1, 16).T, (8, 1))


def rows(idx, k):
    return np.tile(idx, (k, 1))


def look(tab, idx):
    return np.take_along_axis(f64(tab), rows(idx, len(tab)), axis=1)


K, S, V, N, M = 128, 2048, 512, 512, 128


def silu(v):
    return v / (1.0 + np.exp(-v))


def setup_inputs():
    return {"tab": f32(np.random.standard_normal((2, K, S))), "w": bf(np.random.standard_normal((K, M)) / np.sqrt(K)), "offs": striped(np.random.permutation(S)[:N])}


def reference(tab, w, offs):
    idx = offs[:16].T.reshape(-1)
    x = silu(look(tab[0], idx)) * look(tab[1], idx)
    y = f64(w).T @ x
    return y

@@ -1,0 +1,47 @@
+import concourse.mybir as mybir
+
+P = 128
+S = 2048
+N = 512
+PIECE = N // 2
+PER_COLUMN = 16
+
+FLOPS = 2 * P * P * N
+
+BF16, F32, U16 = mybir.dt.bfloat16, mybir.dt.float32, mybir.dt.uint16
+SILU = mybir.ActivationFunctionType.Silu
+MULT = mybir.AluOpType.mult
+
+
+def tile_lookup_glu_silu_none_kernel(tc, tab, w, offs, out):
+    nc = tc.nc
+    with (
+        tc.tile_pool(name="held", bufs=1) as held,
+        tc.tile_pool(name="pieces", bufs=2) as pieces,
+        tc.psum_pool(name="psum", bufs=2) as psum,
+    ):
+        offsets = held.tile([P, N // PER_COLUMN], U16, name="offsets")
+        gate_table = held.tile([P, S], F32, name="gate_table")
+        value_table = held.tile([P, S], F32, name="value_table")
+        weights = held.tile([P, P], BF16, name="weights")
+        gate = held.tile([P, N], F32, name="gate")
+
+        nc.sync.dma_start(offsets[:], offs)
+        nc.sync.dma_start(gate_table[:], tab[0, :, :])
+        nc.sync.dma_start(value_table[:], tab[1, :, :])
+        nc.scalar.dma_start(weights[:], w)
+
+        nc.scalar.activation(gate[:], gate_table[:].indirect(offsets[:]), SILU)
+
+        for start in range(0, N, PIECE):
+            cols = slice(start, start + PIECE)
+            entries = offsets[:, start // PER_COLUMN : (start + PIECE) // PER_COLUMN]
+            product = pieces.tile([P, PIECE], F32, name="product")
+            nc.vector.tensor_tensor(product[:], value_table[:].indirect(entries), gate[:, cols], MULT)
+            x = pieces.tile([P, PIECE], BF16, name="x")
+            nc.scalar.copy(x[:], product[:])
+            y = psum.tile([P, PIECE], F32, name="y")
+            nc.tensor.matmul(y[:], weights[:], x[:], start=True, stop=True)
+            result = pieces.tile([P, PIECE], F32, name="result")
+            nc.vector.tensor_copy(result[:], y[:])
+            nc.sync.dma_start(out[:, cols], result[:])

@@ -25,6 +25,10 @@ def tile_lookup_glu_silu_none_kernel(tc, tab, w, offs, out):
         value_table = held.tile([P, S], F32, name="value_table")
         weights = held.tile([P, P], BF16, name="weights")
         gate = held.tile([P, N], F32, name="gate")
+        warm = held.tile([P, 1], F32, name="warm")
+
+        nc.vector.memset(warm[:], 0.0)
+        nc.scalar.activation(warm[:], warm[:], SILU)
 
         nc.sync.dma_start(offsets[:], offs)
         nc.sync.dma_start(gate_table[:], tab[0, :, :])

@@ -3,7 +3,8 @@ import concourse.mybir as mybir
 P = 128
 S = 2048
 N = 512
-PIECE = N // 2
+PIECE = N // 4
+WARM_UPS = 16
 PER_COLUMN = 16
 
 FLOPS = 2 * P * P * N
@@ -17,23 +18,31 @@ def tile_lookup_glu_silu_none_kernel(tc, tab, w, offs, out):
     nc = tc.nc
     with (
         tc.tile_pool(name="held", bufs=1) as held,
-        tc.tile_pool(name="pieces", bufs=2) as pieces,
-        tc.psum_pool(name="psum", bufs=2) as psum,
+        tc.tile_pool(name="pieces", bufs=N // PIECE) as pieces,
+        tc.psum_pool(name="warm_psum", bufs=1) as warm_psum,
+        tc.psum_pool(name="psum", bufs=N // PIECE) as psum,
     ):
         offsets = held.tile([P, N // PER_COLUMN], U16, name="offsets")
         gate_table = held.tile([P, S], F32, name="gate_table")
         value_table = held.tile([P, S], F32, name="value_table")
         weights = held.tile([P, P], BF16, name="weights")
+        weights_f32 = held.tile([P, P], F32, name="weights_f32")
         gate = held.tile([P, N], F32, name="gate")
         warm = held.tile([P, 1], F32, name="warm")
+        zeros = held.tile([P, N], BF16, name="zeros")
+        warm_y = warm_psum.tile([P, N], F32, name="warm_y")
 
         nc.vector.memset(warm[:], 0.0)
         nc.scalar.activation(warm[:], warm[:], SILU)
+        nc.vector.memset(zeros[:], 0.0)
+        for i in range(WARM_UPS):
+            nc.tensor.matmul(warm_y[:], zeros[:, :P], zeros[:], start=True, stop=True)
 
         nc.sync.dma_start(offsets[:], offs)
         nc.sync.dma_start(gate_table[:], tab[0, :, :])
         nc.sync.dma_start(value_table[:], tab[1, :, :])
         nc.scalar.dma_start(weights[:], w)
+        nc.vector.tensor_copy(weights_f32[:], weights[:])
 
         nc.scalar.activation(gate[:], gate_table[:].indirect(offsets[:]), SILU)
 
@@ -42,10 +51,8 @@ def tile_lookup_glu_silu_none_kernel(tc, tab, w, offs, out):
             entries = offsets[:, start // PER_COLUMN : (start + PIECE) // PER_COLUMN]
             product = pieces.tile([P, PIECE], F32, name="product")
             nc.vector.tensor_tensor(product[:], value_table[:].indirect(entries), gate[:, cols], MULT)
-            x = pieces.tile([P, PIECE], BF16, name="x")
-            nc.scalar.copy(x[:], product[:])
             y = psum.tile([P, PIECE], F32, name="y")
-            nc.tensor.matmul(y[:], weights[:], x[:], start=True, stop=True)
+            nc.tensor.matmul(y[:], weights_f32[:], product[:], start=True, stop=True)
             result = pieces.tile([P, PIECE], F32, name="result")
-            nc.vector.tensor_copy(result[:], y[:])
+            nc.scalar.copy(result[:], y[:])
             nc.sync.dma_start(out[:, cols], result[:])

@@ -38,8 +38,8 @@ def tile_lookup_glu_silu_none_kernel(tc, tab, w, offs, out):
         for i in range(WARM_UPS):
             nc.tensor.matmul(warm_y[:], zeros[:, :P], zeros[:], start=True, stop=True)
 
-        nc.sync.dma_start(offsets[:], offs)
         nc.sync.dma_start(gate_table[:], tab[0, :, :])
+        nc.sync.dma_start(offsets[:], offs)
         nc.sync.dma_start(value_table[:], tab[1, :, :])
         nc.scalar.dma_start(weights[:], w)
         nc.vector.tensor_copy(weights_f32[:], weights[:])
@@ -55,4 +55,4 @@ def tile_lookup_glu_silu_none_kernel(tc, tab, w, offs, out):
             nc.tensor.matmul(y[:], weights_f32[:], product[:], start=True, stop=True)
             result = pieces.tile([P, PIECE], F32, name="result")
             nc.scalar.copy(result[:], y[:])
-            nc.sync.dma_start(out[:, cols], result[:])
+            nc.scalar.dma_start(out[:, cols], result[:])

import concourse.mybir as mybir

P = 128
S = 2048
N = 512
PIECE = N // 4
WARM_UPS = 16
PER_COLUMN = 16

FLOPS = 2 * P * P * N

BF16, F32, U16 = mybir.dt.bfloat16, mybir.dt.float32, mybir.dt.uint16
SILU = mybir.ActivationFunctionType.Silu
MULT = mybir.AluOpType.mult


def tile_lookup_glu_silu_none_kernel(tc, tab, w, offs, out):
    nc = tc.nc
    with (
        tc.tile_pool(name="held", bufs=1) as held,
        tc.tile_pool(name="pieces", bufs=N // PIECE) as pieces,
        tc.psum_pool(name="warm_psum", bufs=1) as warm_psum,
        tc.psum_pool(name="psum", bufs=N // PIECE) as psum,
    ):
        offsets = held.tile([P, N // PER_COLUMN], U16, name="offsets")
        gate_table = held.tile([P, S], F32, name="gate_table")
        value_table = held.tile([P, S], F32, name="value_table")
        weights = held.tile([P, P], BF16, name="weights")
        weights_f32 = held.tile([P, P], F32, name="weights_f32")
        gate = held.tile([P, N], F32, name="gate")
        warm = held.tile([P, 1], F32, name="warm")
        zeros = held.tile([P, N], BF16, name="zeros")
        warm_y = warm_psum.tile([P, N], F32, name="warm_y")

        nc.vector.memset(warm[:], 0.0)
        nc.scalar.activation(warm[:], warm[:], SILU)
        nc.vector.memset(zeros[:], 0.0)
        for i in range(WARM_UPS):
            nc.tensor.matmul(warm_y[:], zeros[:, :P], zeros[:], start=True, stop=True)

        nc.sync.dma_start(gate_table[:], tab[0, :, :])
        nc.sync.dma_start(offsets[:], offs)
        nc.sync.dma_start(value_table[:], tab[1, :, :])
        nc.scalar.dma_start(weights[:], w)
        nc.vector.tensor_copy(weights_f32[:], weights[:])

        nc.scalar.activation(gate[:], gate_table[:].indirect(offsets[:]), SILU)

        for start in range(0, N, PIECE):
            cols = slice(start, start + PIECE)
            entries = offsets[:, start // PER_COLUMN : (start + PIECE) // PER_COLUMN]
            product = pieces.tile([P, PIECE], F32, name="product")
            nc.vector.tensor_tensor(product[:], value_table[:].indirect(entries), gate[:, cols], MULT)
            y = psum.tile([P, PIECE], F32, name="y")
            nc.tensor.matmul(y[:], weights_f32[:], product[:], start=True, stop=True)
            result = pieces.tile([P, PIECE], F32, name="result")
            nc.scalar.copy(result[:], y[:])
            nc.scalar.dma_start(out[:, cols], result[:])
